import numpy as np
import ml_dtypes


def mxq(x, axis, fmt="e4m3"):
    dtype, down = {"e4m3": (ml_dtypes.float8_e4m3fn, 7), "e5m2": (ml_dtypes.float8_e5m2, 14)}[fmt]
    v = np.moveaxis(np.asarray(x, np.float32).astype(ml_dtypes.bfloat16).astype(np.float64), axis, -1)
    blocks = v.reshape(v.shape[:-1] + (-1, 32))
    amax = np.abs(blocks).max(-1, keepdims=True)
    byte = np.maximum(np.where(amax > 0, np.frexp(amax)[1] - 1 + 127, 0) - down, 1)
    scale = np.exp2(byte - 127.0)
    codes = (blocks / scale).astype(np.float32).astype(dtype).astype(np.float64)
    return np.moveaxis((codes * scale).reshape(v.shape), -1, axis)


WIDE = False


def mx_kscale(k):
    if not WIDE:
        return np.ones(k)
    levels = np.array([10, -10, 5, -5, 0])
    if k % 512:
        return np.exp2(np.random.permutation(np.resize(levels, k // 32))).repeat(32)
    a = np.empty((k // 512, 16))
    for p in range(k // 512):
        a[p, :8] = np.random.permutation(np.resize(levels, 8))
        for g in range(8):
            far = levels[np.abs(levels - a[p, g]) >= 10]
            a[p, g + 8] = far[np.random.randint(len(far))]
    return np.exp2(a.ravel()).repeat(32)


def f64(x):
    return np.asarray(x).astype(np.float64)


def striped(idx):
    return np.tile(np.asarray(idx).reshape(-1, 16).T, (8, 1)).astype(np.uint16)


def unstriped(offs):
    return offs[:16].T.reshape(-1).astype(np.int64)


E2M1 = np.array([0.0, 0.5, 1.0, 1.5, 2.0, 3.0, 4.0, 6.0, -0.0, -0.5, -1.0, -1.5, -2.0, -3.0, -4.0, -6.0])


def pack_weight(w, fmt):
    k, n = w.shape
    w = f64(np.asarray(w, np.float32).astype(ml_dtypes.bfloat16)).reshape(k // 32, 32, n)
    amax = np.abs(w).max(1)
    if fmt == "e4m3":
        byte = np.frexp(amax)[1] - 1 + 127 - 7
    else:
        mant, ex = np.frexp(amax / 6.0)
        byte = np.where(mant > 0.5, ex, ex - 1) + 127
    byte = np.clip(np.where(amax > 0, byte, 1), 1, 254)
    scaled = (w * np.exp2(127.0 - byte)[:, None, :]).reshape(k, n).astype(np.float32)
    by_word = np.ascontiguousarray(scaled.reshape(k // 512, 128, 4, n).transpose(0, 1, 3, 2))
    if fmt == "e4m3":
        words = by_word.astype(ml_dtypes.float8_e4m3fn).view(np.uint8)
    else:
        c = by_word.astype(ml_dtypes.float4_e2m1fn).view(np.uint8) & 0xF
        words = (c[..., 0::2] | (c[..., 1::2] << 4)).reshape(k // 512, 128, 2 * n)
    return np.ascontiguousarray(words), np.ascontiguousarray(byte.astype(np.uint8).reshape(k // 512, 16, n))


def unpack_weight(words, scales, fmt):
    g, _, n = scales.shape
    words = np.ascontiguousarray(words).reshape(g, 128, n, -1)
    if fmt == "e4m3":
        vals = words.view(ml_dtypes.float8_e4m3fn).astype(np.float64)
    else:
        nib = np.empty((g, 128, n, 4), np.uint8)
        nib[..., 0::2] = words & 0xF
        nib[..., 1::2] = words >> 4
        vals = E2M1[nib]
    vals = vals * np.repeat(np.exp2(scales.astype(np.float64) - 127.0), 8, axis=1)[..., None]
    return vals.transpose(0, 1, 3, 2).reshape(g * 512, n)


def sgn(shape):
    return np.random.uniform(0.5, 2.0, shape) * np.where(np.random.standard_normal(shape) < 0, -1.0, 1.0)


K, T, J, R, C, O, N = 512, 1024, 256, 512, 512, 256, 256


def setup_inputs():
    n = np.random.standard_normal
    idx = np.random.permutation(T)[:J]
    idx2 = np.random.permutation(C)[:J]
    idx3 = np.random.permutation(C)[:O]
    fk = mx_kscale(K)
    fr = mx_kscale(R)
    xtp = pack_weight(n((K, T)) / fk[:, None], "e2m1")
    wp = pack_weight(n((K, R)) * 1 / np.sqrt(K) * fk[:, None], "e4m3")
    wbp = pack_weight(n((R, N)) * 1 / np.sqrt(R) / fr[:, None], "e2m1")
    return {
        "xt_words": xtp[0],
        "xt_scales": xtp[1],
        "w_words": wp[0],
        "w_scales": wp[1],
        "sa": (np.random.uniform(0.5, 1.6, (R, 1))).astype(np.float32),
        "sg": (0.25 * sgn((R, 1))).astype(np.float32),
        "lo": (np.random.uniform(-0.4, 0.4, (R, 1)) + np.log(fr)[:, None]).astype(np.float32),
        "wb_words": wbp[0],
        "wb_scales": wbp[1],
        "offs": striped(idx),
        "offs2": striped(idx2),
        "offs3": striped(idx3),
    }


def reference(xt_words, xt_scales, w_words, w_scales, sa, sg, lo, wb_words, wb_scales, offs, offs2, offs3):
    idx = unstriped(offs)
    idx2 = unstriped(offs2)
    idx3 = unstriped(offs3)
    xtu = unpack_weight(xt_words, xt_scales, "e2m1")
    wu = unpack_weight(w_words, w_scales, "e4m3")
    wbu = unpack_weight(wb_words, wb_scales, "e2m1")
    xtidxg = xtu[:, idx]
    a = wu.T @ xtidxg
    pw = np.zeros((R, C))
    pw[:, idx2] = a * f64(sa)
    hid = np.exp(pw[:, idx3] * f64(sg) + f64(lo))
    hidq = mxq(hid, 0, "e4m3")
    p = wbu.T @ hidq
    return p

@@ -1,0 +1,164 @@
+from contextlib import ExitStack
+
+import concourse.mybir as mybir
+
+K, T, J, R, C, O, N = 512, 1024, 256, 512, 512, 256, 256
+FLOPS = 2 * K * R * J + 2 * R * N * O
+
+F32 = mybir.dt.float32
+BF16 = mybir.dt.bfloat16
+I32 = mybir.dt.int32
+U32 = mybir.dt.uint32
+U16 = mybir.dt.uint16
+U8 = mybir.dt.uint8
+FP8X4 = mybir.dt.float8_e4m3fn_x4
+FP4X4 = mybir.dt.float4_e2m1fn_x4
+ACT = mybir.ActivationFunctionType
+
+P = 128
+PACK = 4
+QUADS = 4
+HALF = 128
+LIST_COLS = HALF // 16
+
+
+def tile_list_expread_kernel(tc, xt_words, xt_scales, w_words, w_scales, sa, sg, lo, wb_words, wb_scales, offs, offs2, offs3, out):
+    nc = tc.nc
+    with ExitStack() as ctx:
+        sb = ctx.enter_context(tc.tile_pool(name="sb", bufs=1))
+        ps = ctx.enter_context(tc.psum_pool(name="ps", bufs=1))
+
+        token_list = sb.tile([P, J // 16], U16, name="token_list")
+        put_list = sb.tile([P, J // 16], U16, name="put_list")
+        take_list = sb.tile([P, O // 16], U16, name="take_list")
+        xt_codes = sb.tile([P, T], U16, name="xt_codes", align_bytes=64)
+        xt_plane = sb.tile([P, T], U8, name="xt_plane", align_bytes=64)
+        w_raw = sb.tile([P, R], I32, name="w_raw", align_bytes=64)
+        w_rows = sb.tile([PACK, QUADS, R // 4], I32, name="w_rows", align_bytes=64)
+        w_plane_raw = sb.tile([P, R], U8, name="w_plane_raw", align_bytes=64)
+        w_codes = sb.tile([P, R], U32, name="w_codes", align_bytes=64)
+        w_plane = sb.tile([P, R], U8, name="w_plane", align_bytes=64)
+        wb_codes = sb.tile([P, 2 * N], U8, name="wb_codes", align_bytes=64)
+        wb_plane = sb.tile([P, N], U8, name="wb_plane", align_bytes=64)
+        sa_t = sb.tile([P, PACK], F32, name="sa_t")
+        sg_t = sb.tile([P, PACK], F32, name="sg_t")
+        lo_t = sb.tile([P, PACK], F32, name="lo_t")
+        x_codes = sb.tile([P, J], U16, name="x_codes", align_bytes=64)
+        x_plane = sb.tile([P, J], U8, name="x_plane", align_bytes=64)
+        a_sb = [sb.tile([P, J], F32, name="a_sb%d" % t, align_bytes=64) for t in range(PACK)]
+        board = [sb.tile([P, C], F32, name="board%d" % t, align_bytes=64) for t in range(PACK)]
+        hid = sb.tile([P, PACK * O], BF16, name="hid", align_bytes=64)
+        hid_codes = sb.tile([P, O], U32, name="hid_codes", align_bytes=64)
+        hid_plane = sb.tile([P, O], U8, name="hid_plane", align_bytes=64)
+
+        nc.vector.memset(xt_plane[:].bitcast(I32), 0)
+        nc.sync.dma_start(token_list[:], offs)
+        nc.sync.dma_start(w_rows[:], w_scales[0].bitcast(I32).rearrange("(q r) w -> r q w", r=PACK))
+        nc.sync.dma_start(xt_codes[:].bitcast(I32), xt_words[0].bitcast(I32))
+        nc.sync.dma_start(w_raw[:], w_words[0].rearrange("p n t -> p (n t)").bitcast(I32))
+        for q in range(QUADS):
+            queue = nc.sync if q < 2 else nc.scalar
+            queue.dma_start(xt_plane[32 * q : 32 * q + 4, :].bitcast(I32), xt_scales[0][4 * q : 4 * q + 4, :].bitcast(I32))
+        nc.sync.dma_start(put_list[:], offs2)
+        nc.sync.dma_start(sa_t[:], sa.rearrange("(p t) o -> p (t o)", t=PACK))
+        nc.sync.dma_start(take_list[:], offs3)
+        nc.sync.dma_start(sg_t[:], sg.rearrange("(p t) o -> p (t o)", t=PACK))
+        nc.sync.dma_start(lo_t[:], lo.rearrange("(p t) o -> p (t o)", t=PACK))
+        nc.vector.memset(w_plane_raw[:].bitcast(I32), 0)
+        nc.vector.memset(wb_plane[:].bitcast(I32), 0)
+        for t in range(PACK):
+            nc.vector.memset(board[t][:], 0.0)
+        nc.sync.dma_start(wb_codes[:].bitcast(I32), wb_words[0].bitcast(I32))
+        for q in range(QUADS):
+            nc.sync.dma_start(wb_plane[32 * q : 32 * q + 4, :].bitcast(I32), wb_scales[0][4 * q : 4 * q + 4, :].bitcast(I32))
+
+        for q in range(QUADS):
+            nc.vector.tensor_copy(w_plane_raw[32 * q : 32 * q + 4, :].bitcast(I32), w_rows[:, q, :])
+        nc.vector.tensor_copy(
+            w_plane[:].rearrange("p (t m) -> p t m", t=PACK), w_plane_raw[:].rearrange("p (m t) -> p t m", t=PACK)
+        )
+        w_in = w_raw[:].bitcast(U32)
+        nc.scalar.copy(w_codes[:, 0:P], w_in[:, 0:R:PACK])
+        nc.scalar.copy(
+            w_codes[:].rearrange("p (t c i) -> p c t i", t=PACK, i=4)[:, :, 1:PACK, :],
+            w_in.rearrange("p (c i t) -> p c t i", t=PACK, i=4)[:, :, 1:PACK, :],
+        )
+
+        def gather_tokens(h):
+            cols = slice(h * HALF, (h + 1) * HALF)
+            entries = token_list[:, h * LIST_COLS : (h + 1) * LIST_COLS]
+            nc.vector.tensor_copy(x_plane[:, cols], xt_plane[:].indirect(entries))
+            nc.vector.tensor_copy(x_codes[:, cols], xt_codes[:].indirect(entries))
+
+        def first_product(t, j0, j1, tag):
+            acc = ps.tile([P, j1 - j0], F32, name="acc_a", tag=tag)
+            rows = slice(t * P, (t + 1) * P)
+            nc.tensor.matmul_mx(
+                out=acc[:],
+                lhsT=w_codes[:, rows].bitcast(FP8X4),
+                lhsT_scale=w_plane[:, rows],
+                rhs=x_codes[:, j0:j1].bitcast(FP4X4),
+                rhs_scale=x_plane[:, j0:j1],
+                start=True,
+                stop=True,
+            )
+            nc.vector.tensor_copy(a_sb[t][:, j0:j1], acc[:])
+
+        def put(t, j0, j1):
+            nc.scalar.activation(
+                out=board[t][:].indirect(put_list[:, j0 // 16 : j1 // 16]),
+                in_=a_sb[t][:, j0:j1],
+                func=ACT.Copy,
+                scale=sa_t[:, t : t + 1],
+            )
+
+        def take(t, h):
+            nc.scalar.activation(
+                out=hid[:, PACK * HALF * h + t : PACK * HALF * (h + 1) : PACK],
+                in_=board[t][:].indirect(take_list[:, h * LIST_COLS : (h + 1) * LIST_COLS]),
+                func=ACT.Exp,
+                bias=lo_t[:, t : t + 1],
+                scale=sg_t[:, t : t + 1],
+            )
+
+        pieces = [(0, 0, HALF), (1, 0, HALF), (2, 0, J), (3, 0, J), (0, HALF, J), (1, HALF, J)]
+        gather_tokens(0)
+        first_product(0, 0, HALF, "bank0")
+        first_product(1, 0, HALF, "bank1")
+        gather_tokens(1)
+        first_product(2, 0, J, "bank2")
+        first_product(3, 0, J, "bank3")
+        first_product(0, HALF, J, "bank4")
+        first_product(1, HALF, J, "bank5")
+        for piece in pieces:
+            put(*piece)
+
+        out_rows = out.rearrange("(b p) o -> p b o", p=P)
+        for t in (2, 3, 0, 1):
+            for h in range(2):
+                take(t, h)
+        for h in range(2):
+            cols = slice(h * HALF, (h + 1) * HALF)
+            nc.vector.quantize_mx(
+                out=hid_codes[:, cols].bitcast(FP8X4),
+                scales=hid_plane[:, cols],
+                in_=hid[:, PACK * HALF * h : PACK * HALF * (h + 1)],
+            )
+            for b in range(2):
+                acc = ps.tile([P, HALF], F32, name="acc_out", tag="bank%d" % ((6 + b + 2 * h) % 8))
+                nc.tensor.matmul_mx(
+                    out=acc[:],
+                    lhsT=wb_codes[:, 2 * P * b : 2 * P * (b + 1)].bitcast(FP4X4),
+                    lhsT_scale=wb_plane[:, P * b : P * (b + 1)],
+                    rhs=hid_codes[:, cols].bitcast(FP8X4),
+                    rhs_scale=hid_plane[:, cols],
+                    start=True,
+                    stop=True,
+                )
+                res = sb.tile([P, HALF], F32, name="res%d%d" % (h, b), align_bytes=64)
+                if h == 1 and b == 1:
+                    nc.scalar.copy(res[:], acc[:])
+                    nc.scalar.dma_start(out_rows[:, b, cols], res[:])
+                else:
+                    nc.vector.tensor_copy(res[:], acc[:])
+                    nc.sync.dma_start(out_rows[:, b, cols], res[:])

@@ -52,13 +52,13 @@ def tile_list_expread_kernel(tc, xt_words, xt_scales, w_words, w_scales, sa, sg,
         hid_plane = sb.tile([P, O], U8, name="hid_plane", align_bytes=64)
 
         nc.vector.memset(xt_plane[:].bitcast(I32), 0)
-        nc.sync.dma_start(token_list[:], offs)
         nc.sync.dma_start(w_rows[:], w_scales[0].bitcast(I32).rearrange("(q r) w -> r q w", r=PACK))
-        nc.sync.dma_start(xt_codes[:].bitcast(I32), xt_words[0].bitcast(I32))
         nc.sync.dma_start(w_raw[:], w_words[0].rearrange("p n t -> p (n t)").bitcast(I32))
+        nc.sync.dma_start(token_list[:], offs)
         for q in range(QUADS):
-            queue = nc.sync if q < 2 else nc.scalar
+            queue = nc.sync if q == QUADS - 1 else nc.scalar
             queue.dma_start(xt_plane[32 * q : 32 * q + 4, :].bitcast(I32), xt_scales[0][4 * q : 4 * q + 4, :].bitcast(I32))
+        nc.sync.dma_start(xt_codes[:].bitcast(I32), xt_words[0].bitcast(I32))
         nc.sync.dma_start(put_list[:], offs2)
         nc.sync.dma_start(sa_t[:], sa.rearrange("(p t) o -> p (t o)", t=PACK))
         nc.sync.dma_start(take_list[:], offs3)
@@ -78,16 +78,15 @@ def tile_list_expread_kernel(tc, xt_words, xt_scales, w_words, w_scales, sa, sg,
             w_plane[:].rearrange("p (t m) -> p t m", t=PACK), w_plane_raw[:].rearrange("p (m t) -> p t m", t=PACK)
         )
         w_in = w_raw[:].bitcast(U32)
-        nc.scalar.copy(w_codes[:, 0:P], w_in[:, 0:R:PACK])
         nc.scalar.copy(
-            w_codes[:].rearrange("p (t c i) -> p c t i", t=PACK, i=4)[:, :, 1:PACK, :],
-            w_in.rearrange("p (c i t) -> p c t i", t=PACK, i=4)[:, :, 1:PACK, :],
+            w_codes[:].rearrange("p (t c i) -> p c t i", t=PACK, i=4),
+            w_in.rearrange("p (c i t) -> p c t i", t=PACK, i=4),
         )
+        nc.vector.tensor_copy(x_plane[:], xt_plane[:].indirect(token_list[:]))
 
         def gather_tokens(h):
             cols = slice(h * HALF, (h + 1) * HALF)
             entries = token_list[:, h * LIST_COLS : (h + 1) * LIST_COLS]
-            nc.vector.tensor_copy(x_plane[:, cols], xt_plane[:].indirect(entries))
             nc.vector.tensor_copy(x_codes[:, cols], xt_codes[:].indirect(entries))
 
         def first_product(t, j0, j1, tag):
@@ -130,13 +129,16 @@ def tile_list_expread_kernel(tc, xt_words, xt_scales, w_words, w_scales, sa, sg,
         first_product(3, 0, J, "bank3")
         first_product(0, HALF, J, "bank4")
         first_product(1, HALF, J, "bank5")
-        for piece in pieces:
+        for piece in pieces[:4]:
             put(*piece)
+        take(2, 0)
+        put(*pieces[4])
+        take(3, 0)
+        put(*pieces[5])
+        for t, h in ((2, 1), (0, 0), (3, 1), (1, 0), (0, 1), (1, 1)):
+            take(t, h)
 
         out_rows = out.rearrange("(b p) o -> p b o", p=P)
-        for t in (2, 3, 0, 1):
-            for h in range(2):
-                take(t, h)
         for h in range(2):
             cols = slice(h * HALF, (h + 1) * HALF)
             nc.vector.quantize_mx(

from contextlib import ExitStack

import concourse.mybir as mybir

K, T, J, R, C, O, N = 512, 1024, 256, 512, 512, 256, 256
FLOPS = 2 * K * R * J + 2 * R * N * O

F32 = mybir.dt.float32
BF16 = mybir.dt.bfloat16
I32 = mybir.dt.int32
U32 = mybir.dt.uint32
U16 = mybir.dt.uint16
U8 = mybir.dt.uint8
FP8X4 = mybir.dt.float8_e4m3fn_x4
FP4X4 = mybir.dt.float4_e2m1fn_x4
ACT = mybir.ActivationFunctionType

P = 128
PACK = 4
QUADS = 4
HALF = 128
LIST_COLS = HALF // 16


def tile_list_expread_kernel(tc, xt_words, xt_scales, w_words, w_scales, sa, sg, lo, wb_words, wb_scales, offs, offs2, offs3, out):
    nc = tc.nc
    with ExitStack() as ctx:
        sb = ctx.enter_context(tc.tile_pool(name="sb", bufs=1))
        ps = ctx.enter_context(tc.psum_pool(name="ps", bufs=1))

        token_list = sb.tile([P, J // 16], U16, name="token_list")
        put_list = sb.tile([P, J // 16], U16, name="put_list")
        take_list = sb.tile([P, O // 16], U16, name="take_list")
        xt_codes = sb.tile([P, T], U16, name="xt_codes", align_bytes=64)
        xt_plane = sb.tile([P, T], U8, name="xt_plane", align_bytes=64)
        w_raw = sb.tile([P, R], I32, name="w_raw", align_bytes=64)
        w_rows = sb.tile([PACK, QUADS, R // 4], I32, name="w_rows", align_bytes=64)
        w_plane_raw = sb.tile([P, R], U8, name="w_plane_raw", align_bytes=64)
        w_codes = sb.tile([P, R], U32, name="w_codes", align_bytes=64)
        w_plane = sb.tile([P, R], U8, name="w_plane", align_bytes=64)
        wb_codes = sb.tile([P, 2 * N], U8, name="wb_codes", align_bytes=64)
        wb_plane = sb.tile([P, N], U8, name="wb_plane", align_bytes=64)
        sa_t = sb.tile([P, PACK], F32, name="sa_t")
        sg_t = sb.tile([P, PACK], F32, name="sg_t")
        lo_t = sb.tile([P, PACK], F32, name="lo_t")
        x_codes = sb.tile([P, J], U16, name="x_codes", align_bytes=64)
        x_plane = sb.tile([P, J], U8, name="x_plane", align_bytes=64)
        a_sb = [sb.tile([P, J], F32, name="a_sb%d" % t, align_bytes=64) for t in range(PACK)]
        board = [sb.tile([P, C], F32, name="board%d" % t, align_bytes=64) for t in range(PACK)]
        hid = sb.tile([P, PACK * O], BF16, name="hid", align_bytes=64)
        hid_codes = sb.tile([P, O], U32, name="hid_codes", align_bytes=64)
        hid_plane = sb.tile([P, O], U8, name="hid_plane", align_bytes=64)

        nc.vector.memset(xt_plane[:].bitcast(I32), 0)
        nc.sync.dma_start(w_rows[:], w_scales[0].bitcast(I32).rearrange("(q r) w -> r q w", r=PACK))
        nc.sync.dma_start(w_raw[:], w_words[0].rearrange("p n t -> p (n t)").bitcast(I32))
        nc.sync.dma_start(token_list[:], offs)
        for q in range(QUADS):
            queue = nc.sync if q == QUADS - 1 else nc.scalar
            queue.dma_start(xt_plane[32 * q : 32 * q + 4, :].bitcast(I32), xt_scales[0][4 * q : 4 * q + 4, :].bitcast(I32))
        nc.sync.dma_start(xt_codes[:].bitcast(I32), xt_words[0].bitcast(I32))
        nc.sync.dma_start(put_list[:], offs2)
        nc.sync.dma_start(sa_t[:], sa.rearrange("(p t) o -> p (t o)", t=PACK))
        nc.sync.dma_start(take_list[:], offs3)
        nc.sync.dma_start(sg_t[:], sg.rearrange("(p t) o -> p (t o)", t=PACK))
        nc.sync.dma_start(lo_t[:], lo.rearrange("(p t) o -> p (t o)", t=PACK))
        nc.vector.memset(w_plane_raw[:].bitcast(I32), 0)
        nc.vector.memset(wb_plane[:].bitcast(I32), 0)
        for t in range(PACK):
            nc.vector.memset(board[t][:], 0.0)
        nc.sync.dma_start(wb_codes[:].bitcast(I32), wb_words[0].bitcast(I32))
        for q in range(QUADS):
            nc.sync.dma_start(wb_plane[32 * q : 32 * q + 4, :].bitcast(I32), wb_scales[0][4 * q : 4 * q + 4, :].bitcast(I32))

        for q in range(QUADS):
            nc.vector.tensor_copy(w_plane_raw[32 * q : 32 * q + 4, :].bitcast(I32), w_rows[:, q, :])
        nc.vector.tensor_copy(
            w_plane[:].rearrange("p (t m) -> p t m", t=PACK), w_plane_raw[:].rearrange("p (m t) -> p t m", t=PACK)
        )
        w_in = w_raw[:].bitcast(U32)
        nc.scalar.copy(
            w_codes[:].rearrange("p (t c i) -> p c t i", t=PACK, i=4),
            w_in.rearrange("p (c i t) -> p c t i", t=PACK, i=4),
        )
        nc.vector.tensor_copy(x_plane[:], xt_plane[:].indirect(token_list[:]))

        def gather_tokens(h):
            cols = slice(h * HALF, (h + 1) * HALF)
            entries = token_list[:, h * LIST_COLS : (h + 1) * LIST_COLS]
            nc.vector.tensor_copy(x_codes[:, cols], xt_codes[:].indirect(entries))

        def first_product(t, j0, j1, tag):
            acc = ps.tile([P, j1 - j0], F32, name="acc_a", tag=tag)
            rows = slice(t * P, (t + 1) * P)
            nc.tensor.matmul_mx(
                out=acc[:],
                lhsT=w_codes[:, rows].bitcast(FP8X4),
                lhsT_scale=w_plane[:, rows],
                rhs=x_codes[:, j0:j1].bitcast(FP4X4),
                rhs_scale=x_plane[:, j0:j1],
                start=True,
                stop=True,
            )
            nc.vector.tensor_copy(a_sb[t][:, j0:j1], acc[:])

        def put(t, j0, j1):
            nc.scalar.activation(
                out=board[t][:].indirect(put_list[:, j0 // 16 : j1 // 16]),
                in_=a_sb[t][:, j0:j1],
                func=ACT.Copy,
                scale=sa_t[:, t : t + 1],
            )

        def take(t, h):
            nc.scalar.activation(
                out=hid[:, PACK * HALF * h + t : PACK * HALF * (h + 1) : PACK],
                in_=board[t][:].indirect(take_list[:, h * LIST_COLS : (h + 1) * LIST_COLS]),
                func=ACT.Exp,
                bias=lo_t[:, t : t + 1],
                scale=sg_t[:, t : t + 1],
            )

        pieces = [(0, 0, HALF), (1, 0, HALF), (2, 0, J), (3, 0, J), (0, HALF, J), (1, HALF, J)]
        gather_tokens(0)
        first_product(0, 0, HALF, "bank0")
        first_product(1, 0, HALF, "bank1")
        gather_tokens(1)
        first_product(2, 0, J, "bank2")
        first_product(3, 0, J, "bank3")
        first_product(0, HALF, J, "bank4")
        first_product(1, HALF, J, "bank5")
        for piece in pieces[:4]:
            put(*piece)
        take(2, 0)
        put(*pieces[4])
        take(3, 0)
        put(*pieces[5])
        for t, h in ((2, 1), (0, 0), (3, 1), (1, 0), (0, 1), (1, 1)):
            take(t, h)

        out_rows = out.rearrange("(b p) o -> p b o", p=P)
        for h in range(2):
            cols = slice(h * HALF, (h + 1) * HALF)
            nc.vector.quantize_mx(
                out=hid_codes[:, cols].bitcast(FP8X4),
                scales=hid_plane[:, cols],
                in_=hid[:, PACK * HALF * h : PACK * HALF * (h + 1)],
            )
            for b in range(2):
                acc = ps.tile([P, HALF], F32, name="acc_out", tag="bank%d" % ((6 + b + 2 * h) % 8))
                nc.tensor.matmul_mx(
                    out=acc[:],
                    lhsT=wb_codes[:, 2 * P * b : 2 * P * (b + 1)].bitcast(FP4X4),
                    lhsT_scale=wb_plane[:, P * b : P * (b + 1)],
                    rhs=hid_codes[:, cols].bitcast(FP8X4),
                    rhs_scale=hid_plane[:, cols],
                    start=True,
                    stop=True,
                )
                res = sb.tile([P, HALF], F32, name="res%d%d" % (h, b), align_bytes=64)
                if h == 1 and b == 1:
                    nc.scalar.copy(res[:], acc[:])
                    nc.scalar.dma_start(out_rows[:, b, cols], res[:])
                else:
                    nc.vector.tensor_copy(res[:], acc[:])
                    nc.sync.dma_start(out_rows[:, b, cols], res[:])
